import numpy as np
import ml_dtypes


def mxq(x, axis, fmt="e4m3"):
    dtype, down = {"e4m3": (ml_dtypes.float8_e4m3fn, 7), "e5m2": (ml_dtypes.float8_e5m2, 14)}[fmt]
    v = np.moveaxis(np.asarray(x, np.float32).astype(ml_dtypes.bfloat16).astype(np.float64), axis, -1)
    blocks = v.reshape(v.shape[:-1] + (-1, 32))
    amax = np.abs(blocks).max(-1, keepdims=True)
    byte = np.maximum(np.where(amax > 0, np.frexp(amax)[1] - 1 + 127, 0) - down, 1)
    scale = np.exp2(byte - 127.0)
    codes = (blocks / scale).astype(np.float32).astype(dtype).astype(np.float64)
    return np.moveaxis((codes * scale).reshape(v.shape), -1, axis)


WIDE = False


def mx_kscale(k):
    if not WIDE:
        return np.ones(k)
    levels = np.array([10, -10, 5, -5, 0])
    if k % 512:
        return np.exp2(np.random.permutation(np.resize(levels, k // 32))).repeat(32)
    a = np.empty((k // 512, 16))
    for p in range(k // 512):
        a[p, :8] = np.random.permutation(np.resize(levels, 8))
        for g in range(8):
            far = levels[np.abs(levels - a[p, g]) >= 10]
            a[p, g + 8] = far[np.random.randint(len(far))]
    return np.exp2(a.ravel()).repeat(32)


def f64(x):
    return np.asarray(x).astype(np.float64)


def striped(idx):
    return np.tile(np.asarray(idx).reshape(-1, 16).T, (8, 1)).astype(np.uint16)


def unstriped(offs):
    return offs[:16].T.reshape(-1).astype(np.int64)


E2M1 = np.array([0.0, 0.5, 1.0, 1.5, 2.0, 3.0, 4.0, 6.0, -0.0, -0.5, -1.0, -1.5, -2.0, -3.0, -4.0, -6.0])


def pack_weight(w, fmt):
    k, n = w.shape
    w = f64(np.asarray(w, np.float32).astype(ml_dtypes.bfloat16)).reshape(k // 32, 32, n)
    amax = np.abs(w).max(1)
    if fmt == "e4m3":
        byte = np.frexp(amax)[1] - 1 + 127 - 7
    else:
        mant, ex = np.frexp(amax / 6.0)
        byte = np.where(mant > 0.5, ex, ex - 1) + 127
    byte = np.clip(np.where(amax > 0, byte, 1), 1, 254)
    scaled = (w * np.exp2(127.0 - byte)[:, None, :]).reshape(k, n).astype(np.float32)
    by_word = np.ascontiguousarray(scaled.reshape(k // 512, 128, 4, n).transpose(0, 1, 3, 2))
    if fmt == "e4m3":
        words = by_word.astype(ml_dtypes.float8_e4m3fn).view(np.uint8)
    else:
        c = by_word.astype(ml_dtypes.float4_e2m1fn).view(np.uint8) & 0xF
        words = (c[..., 0::2] | (c[..., 1::2] << 4)).reshape(k // 512, 128, 2 * n)
    return np.ascontiguousarray(words), np.ascontiguousarray(byte.astype(np.uint8).reshape(k // 512, 16, n))


def unpack_weight(words, scales, fmt):
    g, _, n = scales.shape
    words = np.ascontiguousarray(words).reshape(g, 128, n, -1)
    if fmt == "e4m3":
        vals = words.view(ml_dtypes.float8_e4m3fn).astype(np.float64)
    else:
        nib = np.empty((g, 128, n, 4), np.uint8)
        nib[..., 0::2] = words & 0xF
        nib[..., 1::2] = words >> 4
        vals = E2M1[nib]
    vals = vals * np.repeat(np.exp2(scales.astype(np.float64) - 127.0), 8, axis=1)[..., None]
    return vals.transpose(0, 1, 3, 2).reshape(g * 512, n)


def softplus(v):
    return np.log(1.0 + np.exp(v))


def sigmoid(v):
    return 1.0 / (1.0 + np.exp(-v))


D, E, T, I, Q = 512, 512, 2048, 512, 128


def setup_inputs():
    n = np.random.standard_normal
    idx = np.random.permutation(T)[:I]
    fd = mx_kscale(D)
    fe = mx_kscale(E)
    keysp = pack_weight(n((D, T)) / fd[:, None], "e4m3")
    valsp = pack_weight(n((E, T)) / fe[:, None], "e4m3")
    return {
        "query": (n((D, Q)) * 1.0 / np.sqrt(D) * fd[:, None]).astype(np.float32),
        "keys_words": keysp[0],
        "keys_scales": keysp[1],
        "th": (np.random.uniform(-0.5, 0.5, (Q, 1))).astype(np.float32),
        "reserve": (np.random.uniform(20.0, 100.0, (Q, 1))).astype(np.float32),
        "gout": (n((E, Q)) * 1 / np.sqrt(E) * fe[:, None]).astype(np.float32),
        "vals_words": valsp[0],
        "vals_scales": valsp[1],
        "size": (np.random.uniform(0.5, 2.0, (1, I))).astype(np.float32),
        "old": (0.5 * n((Q, T))).astype(np.float32),
        "offs": striped(idx),
    }


def reference(query, keys_words, keys_scales, th, reserve, gout, vals_words, vals_scales, size, old, offs):
    idx = unstriped(offs)
    keysu = unpack_weight(keys_words, keys_scales, "e4m3")
    valsu = unpack_weight(vals_words, vals_scales, "e4m3")
    queryq = mxq(f64(query), 0, "e4m3")
    keysidxg = keysu[:, idx]
    a = queryq.T @ keysidxg
    p = softplus(a - f64(th))
    z = np.sum(p, axis=1, keepdims=True) + f64(reserve)
    goutq = mxq(f64(gout), 0, "e4m3")
    valsidxg = valsu[:, idx]
    c0 = goutq.T @ valsidxg
    dz = np.sum(c0 * p * f64(size) / np.square(z) * (-1.0), axis=1, keepdims=True)
    dp = c0 / z * f64(size) + dz
    da = dp * sigmoid(a - f64(th))
    gs = da * 512.0
    gf = np.zeros((Q, T))
    gf[:, idx] = gs
    y = f64(old) + gf
    return y

@@ -1,0 +1,158 @@
+from contextlib import ExitStack
+
+import concourse.mybir as mybir
+from concourse.masks import make_identity
+
+F32 = mybir.dt.float32
+BF16 = mybir.dt.bfloat16
+I32 = mybir.dt.int32
+U32 = mybir.dt.uint32
+U16 = mybir.dt.uint16
+U8 = mybir.dt.uint8
+FP8X4 = mybir.dt.float8_e4m3fn_x4
+ALU = mybir.AluOpType
+ACT = mybir.ActivationFunctionType
+
+P = 128
+PACK = 4
+D, E, T, SLOTS, Q = 512, 512, 2048, 512, 128
+HALF = SLOTS // 2
+PER_COLUMN = 16
+GAIN = 512.0
+FLOOR = 2.0 ** -60
+CHUNKS = (512, 640, 576, 320)
+
+FLOPS = 2 * Q * SLOTS * (D + E)
+
+
+def tile_attend_bsoftthreshold_s_kernel(tc, query, keys_words, keys_scales, th, reserve, gout,
+                                         vals_words, vals_scales, size, old, offs, out):
+    nc = tc.nc
+    with ExitStack() as ctx:
+        sb = ctx.enter_context(tc.tile_pool(name="sb", bufs=1))
+        ps = ctx.enter_context(tc.psum_pool(name="ps", bufs=1))
+
+        offsets = sb.tile([P, SLOTS // PER_COLUMN], U16, name="offsets")
+        nc.sync.dma_start(offsets[:], offs)
+
+        def cleared_window(name):
+            window = sb.tile([P, T], U8, name=name, align_bytes=64)
+            nc.gpsimd.memset(window[:].bitcast(I32), 0)
+            return window
+
+        def load_scales(scales, window):
+            rows = scales[0].bitcast(I32)
+            for r in range(4):
+                nc.sync.dma_start(window[r:P:32, :].bitcast(I32), rows[r:16:4, :])
+
+        def load_words(words, name):
+            window = sb.tile([P, T], U32, name=name, align_bytes=64)
+            nc.sync.dma_start(window[:].bitcast(I32), words[0].rearrange("p n t -> p (n t)").bitcast(I32))
+            return window
+
+        def load_rows(x, name):
+            raw = sb.tile([P, PACK, Q], F32, name=name)
+            nc.sync.dma_start(raw[:], x.rearrange("(p j) q -> p j q", j=PACK))
+            return raw
+
+        def quantise(raw, negate, name):
+            grouped = sb.tile([P, Q, PACK], BF16, name=name + "_bf16", align_bytes=64)
+            if negate:
+                nc.vector.tensor_scalar(grouped[:], raw[:].rearrange("p j q -> p q j"), -1.0, None, ALU.mult)
+            else:
+                nc.scalar.copy(grouped[:], raw[:].rearrange("p j q -> p q j"))
+            codes = sb.tile([P, Q], U32, name=name + "_codes", align_bytes=64)
+            planes = sb.tile([P, Q], U8, name=name + "_scales", align_bytes=64)
+            nc.vector.quantize_mx(out=codes[:].bitcast(FP8X4), scales=planes[:],
+                                  in_=grouped[:].rearrange("p q j -> p (q j)"))
+            return codes, planes
+
+        def gather_scales(window, name):
+            listed = sb.tile([P, SLOTS], U8, name=name, align_bytes=64)
+            nc.vector.tensor_copy(listed[:], window[:].indirect(offsets[:]))
+            return listed
+
+        def listed_product(codes, planes, window, listed_scales, name, tag):
+            listed = sb.tile([P, SLOTS], U32, name=name + "_words", align_bytes=64)
+            bank = ps.tile([P, SLOTS], F32, name=name, tag=tag)
+            for h in range(2):
+                cols = slice(h * HALF, (h + 1) * HALF)
+                entries = slice(h * HALF // PER_COLUMN, (h + 1) * HALF // PER_COLUMN)
+                nc.vector.tensor_copy(listed[:, cols], window[:].indirect(offsets[:, entries]))
+                nc.tensor.matmul_mx(out=bank[:, cols], lhsT=codes[:].bitcast(FP8X4), lhsT_scale=planes[:],
+                                    rhs=listed[:, cols].bitcast(FP8X4), rhs_scale=listed_scales[:, cols],
+                                    start=True, stop=True)
+            return bank
+
+        keys_scale_window = cleared_window("keys_scale_window")
+        vals_scale_window = cleared_window("vals_scale_window")
+        ident = sb.tile([P, P], F32, name="ident")
+        make_identity(nc, ident[:])
+        floor = sb.tile([P, 1], F32, name="floor")
+        nc.vector.memset(floor[:], FLOOR)
+        placed = sb.tile([P, T], F32, name="placed")
+        nc.vector.memset(placed[:], 0.0)
+
+        size_cols = sb.tile([P, PACK], F32, name="size_cols")
+        nc.scalar.dma_start(size_cols[:], size.rearrange("o (p j) -> (o p) j", j=PACK))
+        query_raw = load_rows(query, "query_raw")
+        load_scales(keys_scales, keys_scale_window)
+        keys_window = load_words(keys_words, "keys_window")
+        th_sb = sb.tile([P, 1], F32, name="th_sb")
+        nc.sync.dma_start(th_sb[:], th)
+        load_scales(vals_scales, vals_scale_window)
+        gout_raw = load_rows(gout, "gout_raw")
+        vals_window = load_words(vals_words, "vals_window")
+        reserve_sb = sb.tile([P, 1], F32, name="reserve_sb")
+        nc.sync.dma_start(reserve_sb[:], reserve)
+        old_sb = sb.tile([P, T], F32, name="old_sb")
+        nc.sync.dma_start(old_sb[:], old)
+
+        warm = sb.tile([P, 1], F32, name="warm")
+        nc.scalar.activation(warm[:], floor[:], ACT.Sigmoid)
+        size_bank = ps.tile([P, PACK, P], F32, name="size_bank", tag="first_bank")
+        for j in range(PACK):
+            nc.tensor.transpose(size_bank[:, j, :], size_cols[:, j:j + 1].to_broadcast([P, P]), ident[:])
+        size_rows = sb.tile([P, SLOTS], F32, name="size_rows")
+        nc.scalar.copy(size_rows[:].rearrange("p (n j) -> p n j", j=PACK), size_bank[:].rearrange("p j n -> p n j"))
+
+        query_codes, query_planes = quantise(query_raw, True, "query")
+        keys_listed_scales = gather_scales(keys_scale_window, "keys_listed_scales")
+        neg_a = listed_product(query_codes, query_planes, keys_window, keys_listed_scales, "neg_a", "first_bank")
+        vals_listed_scales = gather_scales(vals_scale_window, "vals_listed_scales")
+        gout_codes, gout_planes = quantise(gout_raw, False, "gout")
+
+        rest = sb.tile([P, SLOTS], F32, name="rest")
+        nc.scalar.activation(rest[:], neg_a[:], ACT.Sigmoid, bias=th_sb[:], scale=1.0)
+        log_rest = sb.tile([P, SLOTS], F32, name="log_rest")
+        nc.scalar.activation(log_rest[:], rest[:], ACT.Ln, bias=floor[:], scale=1.0)
+        slope = sb.tile([P, SLOTS], F32, name="slope")
+        nc.scalar.activation(slope[:], rest[:], ACT.Copy, bias=GAIN, scale=-GAIN)
+
+        c0 = listed_product(gout_codes, gout_planes, vals_window, vals_listed_scales, "c0", "second_bank")
+
+        neg_p = sb.tile([P, SLOTS], F32, name="neg_p")
+        neg_sum = sb.tile([P, 1], F32, name="neg_sum")
+        nc.vector.scalar_tensor_tensor(neg_p[:], neg_a[:], th_sb[:], log_rest[:], ALU.add, ALU.min, accum_out=neg_sum[:])
+        z = sb.tile([P, 1], F32, name="z")
+        nc.vector.tensor_tensor(z[:], reserve_sb[:], neg_sum[:], ALU.subtract)
+        weighted = sb.tile([P, SLOTS], F32, name="weighted")
+        nc.vector.tensor_tensor(weighted[:, :HALF], c0[:, :HALF], size_rows[:, :HALF], ALU.mult)
+        inv_z = sb.tile([P, 1], F32, name="inv_z")
+        nc.vector.reciprocal(inv_z[:], z[:])
+        nc.vector.tensor_tensor(weighted[:, HALF:], c0[:, HALF:], size_rows[:, HALF:], ALU.mult)
+        terms = sb.tile([P, SLOTS], F32, name="terms")
+        shift = sb.tile([P, 1], F32, name="shift")
+        nc.vector.scalar_tensor_tensor(terms[:], weighted[:], inv_z[:], neg_p[:], ALU.mult, ALU.mult, accum_out=shift[:])
+        dp = sb.tile([P, SLOTS], F32, name="dp")
+        nc.vector.tensor_scalar(dp[:], weighted[:], shift[:], inv_z[:], ALU.add, ALU.mult)
+        nc.vector.tensor_tensor(placed[:].indirect(offsets[:]), dp[:], slope[:], ALU.mult)
+
+        result = sb.tile([P, T], F32, name="result")
+        start = 0
+        for n, width in enumerate(CHUNKS):
+            cols = slice(start, start + width)
+            nc.vector.tensor_tensor(result[:, cols], old_sb[:, cols], placed[:, cols], ALU.add)
+            queue = nc.sync if n % 2 == 0 else nc.scalar
+            queue.dma_start(out[:, cols], result[:, cols])
+            start += width

@@ -1,7 +1,6 @@
 from contextlib import ExitStack
 
 import concourse.mybir as mybir
-from concourse.masks import make_identity
 
 F32 = mybir.dt.float32
 BF16 = mybir.dt.bfloat16
@@ -46,21 +45,18 @@ def tile_attend_bsoftthreshold_s_kernel(tc, query, keys_words, keys_scales, th, 
                 nc.sync.dma_start(window[r:P:32, :].bitcast(I32), rows[r:16:4, :])
 
         def load_words(words, name):
-            window = sb.tile([P, T], U32, name=name, align_bytes=64)
+            window = sb.tile([P, T], U32, name=name, tag=name, align_bytes=64)
             nc.sync.dma_start(window[:].bitcast(I32), words[0].rearrange("p n t -> p (n t)").bitcast(I32))
             return window
 
         def load_rows(x, name):
-            raw = sb.tile([P, PACK, Q], F32, name=name)
+            raw = sb.tile([P, PACK, Q], F32, name=name, tag=name)
             nc.sync.dma_start(raw[:], x.rearrange("(p j) q -> p j q", j=PACK))
             return raw
 
-        def quantise(raw, negate, name):
-            grouped = sb.tile([P, Q, PACK], BF16, name=name + "_bf16", align_bytes=64)
-            if negate:
-                nc.vector.tensor_scalar(grouped[:], raw[:].rearrange("p j q -> p q j"), -1.0, None, ALU.mult)
-            else:
-                nc.scalar.copy(grouped[:], raw[:].rearrange("p j q -> p q j"))
+        def quantise(raw, sign, name, tag):
+            grouped = sb.tile([P, Q, PACK], BF16, name=name + "_bf16", tag=tag, align_bytes=64)
+            nc.scalar.activation(grouped[:], raw[:].rearrange("p j q -> p q j"), ACT.Copy, scale=sign)
             codes = sb.tile([P, Q], U32, name=name + "_codes", align_bytes=64)
             planes = sb.tile([P, Q], U8, name=name + "_scales", align_bytes=64)
             nc.vector.quantize_mx(out=codes[:].bitcast(FP8X4), scales=planes[:],
@@ -72,8 +68,8 @@ def tile_attend_bsoftthreshold_s_kernel(tc, query, keys_words, keys_scales, th, 
             nc.vector.tensor_copy(listed[:], window[:].indirect(offsets[:]))
             return listed
 
-        def listed_product(codes, planes, window, listed_scales, name, tag):
-            listed = sb.tile([P, SLOTS], U32, name=name + "_words", align_bytes=64)
+        def listed_product(codes, planes, window, listed_scales, name, tag, words_tag):
+            listed = sb.tile([P, SLOTS], U32, name=name + "_words", tag=words_tag, align_bytes=64)
             bank = ps.tile([P, SLOTS], F32, name=name, tag=tag)
             for h in range(2):
                 cols = slice(h * HALF, (h + 1) * HALF)
@@ -85,23 +81,26 @@ def tile_attend_bsoftthreshold_s_kernel(tc, query, keys_words, keys_scales, th, 
             return bank
 
         keys_scale_window = cleared_window("keys_scale_window")
-        vals_scale_window = cleared_window("vals_scale_window")
-        ident = sb.tile([P, P], F32, name="ident")
-        make_identity(nc, ident[:])
         floor = sb.tile([P, 1], F32, name="floor")
         nc.vector.memset(floor[:], FLOOR)
-        placed = sb.tile([P, T], F32, name="placed")
-        nc.vector.memset(placed[:], 0.0)
+        vals_scale_window = cleared_window("vals_scale_window")
+        ident = sb.tile([P, P], F32, name="ident")
+        zeros = sb.tile([P, P], F32, name="zeros", tag="zeros_then_placed")
+        nc.gpsimd.memset(zeros[:], 0.0)
+        nc.gpsimd.affine_select(out=ident[:], in_=zeros[:], compare_op=ALU.not_equal, fill=1.0, base=0,
+                                pattern=[[-1, P]], channel_multiplier=1)
+        placed = sb.tile([P, T], F32, name="placed", tag="zeros_then_placed")
+        nc.gpsimd.memset(placed[:], 0.0)
 
-        size_cols = sb.tile([P, PACK], F32, name="size_cols")
+        size_cols = sb.tile([P, PACK], F32, name="size_cols", tag="staging", align_bytes=64)
         nc.scalar.dma_start(size_cols[:], size.rearrange("o (p j) -> (o p) j", j=PACK))
         query_raw = load_rows(query, "query_raw")
         load_scales(keys_scales, keys_scale_window)
         keys_window = load_words(keys_words, "keys_window")
         th_sb = sb.tile([P, 1], F32, name="th_sb")
         nc.sync.dma_start(th_sb[:], th)
-        load_scales(vals_scales, vals_scale_window)
         gout_raw = load_rows(gout, "gout_raw")
+        load_scales(vals_scales, vals_scale_window)
         vals_window = load_words(vals_words, "vals_window")
         reserve_sb = sb.tile([P, 1], F32, name="reserve_sb")
         nc.sync.dma_start(reserve_sb[:], reserve)
@@ -113,34 +112,33 @@ def tile_attend_bsoftthreshold_s_kernel(tc, query, keys_words, keys_scales, th, 
         size_bank = ps.tile([P, PACK, P], F32, name="size_bank", tag="first_bank")
         for j in range(PACK):
             nc.tensor.transpose(size_bank[:, j, :], size_cols[:, j:j + 1].to_broadcast([P, P]), ident[:])
+        query_codes, query_planes = quantise(query_raw, -1.0, "query", "query_bf16")
         size_rows = sb.tile([P, SLOTS], F32, name="size_rows")
         nc.scalar.copy(size_rows[:].rearrange("p (n j) -> p n j", j=PACK), size_bank[:].rearrange("p j n -> p n j"))
-
-        query_codes, query_planes = quantise(query_raw, True, "query")
         keys_listed_scales = gather_scales(keys_scale_window, "keys_listed_scales")
-        neg_a = listed_product(query_codes, query_planes, keys_window, keys_listed_scales, "neg_a", "first_bank")
+        neg_a = listed_product(query_codes, query_planes, keys_window, keys_listed_scales, "neg_a", "first_bank", "keys_listed")
         vals_listed_scales = gather_scales(vals_scale_window, "vals_listed_scales")
-        gout_codes, gout_planes = quantise(gout_raw, False, "gout")
+        gout_codes, gout_planes = quantise(gout_raw, 1.0, "gout", "staging")
 
-        rest = sb.tile([P, SLOTS], F32, name="rest")
+        rest = sb.tile([P, SLOTS], F32, name="rest", tag="gout_raw")
         nc.scalar.activation(rest[:], neg_a[:], ACT.Sigmoid, bias=th_sb[:], scale=1.0)
         log_rest = sb.tile([P, SLOTS], F32, name="log_rest")
         nc.scalar.activation(log_rest[:], rest[:], ACT.Ln, bias=floor[:], scale=1.0)
         slope = sb.tile([P, SLOTS], F32, name="slope")
         nc.scalar.activation(slope[:], rest[:], ACT.Copy, bias=GAIN, scale=-GAIN)
 
-        c0 = listed_product(gout_codes, gout_planes, vals_window, vals_listed_scales, "c0", "second_bank")
+        c0 = listed_product(gout_codes, gout_planes, vals_window, vals_listed_scales, "c0", "second_bank", "staging")
 
-        neg_p = sb.tile([P, SLOTS], F32, name="neg_p")
+        neg_p = sb.tile([P, SLOTS], F32, name="neg_p", tag="vals_window", align_bytes=64)
         neg_sum = sb.tile([P, 1], F32, name="neg_sum")
         nc.vector.scalar_tensor_tensor(neg_p[:], neg_a[:], th_sb[:], log_rest[:], ALU.add, ALU.min, accum_out=neg_sum[:])
-        z = sb.tile([P, 1], F32, name="z")
-        nc.vector.tensor_tensor(z[:], reserve_sb[:], neg_sum[:], ALU.subtract)
         weighted = sb.tile([P, SLOTS], F32, name="weighted")
         nc.vector.tensor_tensor(weighted[:, :HALF], c0[:, :HALF], size_rows[:, :HALF], ALU.mult)
+        z = sb.tile([P, 1], F32, name="z")
+        nc.vector.tensor_tensor(z[:], reserve_sb[:], neg_sum[:], ALU.subtract)
+        nc.vector.tensor_tensor(weighted[:, HALF:], c0[:, HALF:], size_rows[:, HALF:], ALU.mult)
         inv_z = sb.tile([P, 1], F32, name="inv_z")
         nc.vector.reciprocal(inv_z[:], z[:])
-        nc.vector.tensor_tensor(weighted[:, HALF:], c0[:, HALF:], size_rows[:, HALF:], ALU.mult)
         terms = sb.tile([P, SLOTS], F32, name="terms")
         shift = sb.tile([P, 1], F32, name="shift")
         nc.vector.scalar_tensor_tensor(terms[:], weighted[:], inv_z[:], neg_p[:], ALU.mult, ALU.mult, accum_out=shift[:])

from contextlib import ExitStack

import concourse.mybir as mybir

F32 = mybir.dt.float32
BF16 = mybir.dt.bfloat16
I32 = mybir.dt.int32
U32 = mybir.dt.uint32
U16 = mybir.dt.uint16
U8 = mybir.dt.uint8
FP8X4 = mybir.dt.float8_e4m3fn_x4
ALU = mybir.AluOpType
ACT = mybir.ActivationFunctionType

P = 128
PACK = 4
D, E, T, SLOTS, Q = 512, 512, 2048, 512, 128
HALF = SLOTS // 2
PER_COLUMN = 16
GAIN = 512.0
FLOOR = 2.0 ** -60
CHUNKS = (512, 640, 576, 320)

FLOPS = 2 * Q * SLOTS * (D + E)


def tile_attend_bsoftthreshold_s_kernel(tc, query, keys_words, keys_scales, th, reserve, gout,
                                         vals_words, vals_scales, size, old, offs, out):
    nc = tc.nc
    with ExitStack() as ctx:
        sb = ctx.enter_context(tc.tile_pool(name="sb", bufs=1))
        ps = ctx.enter_context(tc.psum_pool(name="ps", bufs=1))

        offsets = sb.tile([P, SLOTS // PER_COLUMN], U16, name="offsets")
        nc.sync.dma_start(offsets[:], offs)

        def cleared_window(name):
            window = sb.tile([P, T], U8, name=name, align_bytes=64)
            nc.gpsimd.memset(window[:].bitcast(I32), 0)
            return window

        def load_scales(scales, window):
            rows = scales[0].bitcast(I32)
            for r in range(4):
                nc.sync.dma_start(window[r:P:32, :].bitcast(I32), rows[r:16:4, :])

        def load_words(words, name):
            window = sb.tile([P, T], U32, name=name, tag=name, align_bytes=64)
            nc.sync.dma_start(window[:].bitcast(I32), words[0].rearrange("p n t -> p (n t)").bitcast(I32))
            return window

        def load_rows(x, name):
            raw = sb.tile([P, PACK, Q], F32, name=name, tag=name)
            nc.sync.dma_start(raw[:], x.rearrange("(p j) q -> p j q", j=PACK))
            return raw

        def quantise(raw, sign, name, tag):
            grouped = sb.tile([P, Q, PACK], BF16, name=name + "_bf16", tag=tag, align_bytes=64)
            nc.scalar.activation(grouped[:], raw[:].rearrange("p j q -> p q j"), ACT.Copy, scale=sign)
            codes = sb.tile([P, Q], U32, name=name + "_codes", align_bytes=64)
            planes = sb.tile([P, Q], U8, name=name + "_scales", align_bytes=64)
            nc.vector.quantize_mx(out=codes[:].bitcast(FP8X4), scales=planes[:],
                                  in_=grouped[:].rearrange("p q j -> p (q j)"))
            return codes, planes

        def gather_scales(window, name):
            listed = sb.tile([P, SLOTS], U8, name=name, align_bytes=64)
            nc.vector.tensor_copy(listed[:], window[:].indirect(offsets[:]))
            return listed

        def listed_product(codes, planes, window, listed_scales, name, tag, words_tag):
            listed = sb.tile([P, SLOTS], U32, name=name + "_words", tag=words_tag, align_bytes=64)
            bank = ps.tile([P, SLOTS], F32, name=name, tag=tag)
            for h in range(2):
                cols = slice(h * HALF, (h + 1) * HALF)
                entries = slice(h * HALF // PER_COLUMN, (h + 1) * HALF // PER_COLUMN)
                nc.vector.tensor_copy(listed[:, cols], window[:].indirect(offsets[:, entries]))
                nc.tensor.matmul_mx(out=bank[:, cols], lhsT=codes[:].bitcast(FP8X4), lhsT_scale=planes[:],
                                    rhs=listed[:, cols].bitcast(FP8X4), rhs_scale=listed_scales[:, cols],
                                    start=True, stop=True)
            return bank

        keys_scale_window = cleared_window("keys_scale_window")
        floor = sb.tile([P, 1], F32, name="floor")
        nc.vector.memset(floor[:], FLOOR)
        vals_scale_window = cleared_window("vals_scale_window")
        ident = sb.tile([P, P], F32, name="ident")
        zeros = sb.tile([P, P], F32, name="zeros", tag="zeros_then_placed")
        nc.gpsimd.memset(zeros[:], 0.0)
        nc.gpsimd.affine_select(out=ident[:], in_=zeros[:], compare_op=ALU.not_equal, fill=1.0, base=0,
                                pattern=[[-1, P]], channel_multiplier=1)
        placed = sb.tile([P, T], F32, name="placed", tag="zeros_then_placed")
        nc.gpsimd.memset(placed[:], 0.0)

        size_cols = sb.tile([P, PACK], F32, name="size_cols", tag="staging", align_bytes=64)
        nc.scalar.dma_start(size_cols[:], size.rearrange("o (p j) -> (o p) j", j=PACK))
        query_raw = load_rows(query, "query_raw")
        load_scales(keys_scales, keys_scale_window)
        keys_window = load_words(keys_words, "keys_window")
        th_sb = sb.tile([P, 1], F32, name="th_sb")
        nc.sync.dma_start(th_sb[:], th)
        gout_raw = load_rows(gout, "gout_raw")
        load_scales(vals_scales, vals_scale_window)
        vals_window = load_words(vals_words, "vals_window")
        reserve_sb = sb.tile([P, 1], F32, name="reserve_sb")
        nc.sync.dma_start(reserve_sb[:], reserve)
        old_sb = sb.tile([P, T], F32, name="old_sb")
        nc.sync.dma_start(old_sb[:], old)

        warm = sb.tile([P, 1], F32, name="warm")
        nc.scalar.activation(warm[:], floor[:], ACT.Sigmoid)
        size_bank = ps.tile([P, PACK, P], F32, name="size_bank", tag="first_bank")
        for j in range(PACK):
            nc.tensor.transpose(size_bank[:, j, :], size_cols[:, j:j + 1].to_broadcast([P, P]), ident[:])
        query_codes, query_planes = quantise(query_raw, -1.0, "query", "query_bf16")
        size_rows = sb.tile([P, SLOTS], F32, name="size_rows")
        nc.scalar.copy(size_rows[:].rearrange("p (n j) -> p n j", j=PACK), size_bank[:].rearrange("p j n -> p n j"))
        keys_listed_scales = gather_scales(keys_scale_window, "keys_listed_scales")
        neg_a = listed_product(query_codes, query_planes, keys_window, keys_listed_scales, "neg_a", "first_bank", "keys_listed")
        vals_listed_scales = gather_scales(vals_scale_window, "vals_listed_scales")
        gout_codes, gout_planes = quantise(gout_raw, 1.0, "gout", "staging")

        rest = sb.tile([P, SLOTS], F32, name="rest", tag="gout_raw")
        nc.scalar.activation(rest[:], neg_a[:], ACT.Sigmoid, bias=th_sb[:], scale=1.0)
        log_rest = sb.tile([P, SLOTS], F32, name="log_rest")
        nc.scalar.activation(log_rest[:], rest[:], ACT.Ln, bias=floor[:], scale=1.0)
        slope = sb.tile([P, SLOTS], F32, name="slope")
        nc.scalar.activation(slope[:], rest[:], ACT.Copy, bias=GAIN, scale=-GAIN)

        c0 = listed_product(gout_codes, gout_planes, vals_window, vals_listed_scales, "c0", "second_bank", "staging")

        neg_p = sb.tile([P, SLOTS], F32, name="neg_p", tag="vals_window", align_bytes=64)
        neg_sum = sb.tile([P, 1], F32, name="neg_sum")
        nc.vector.scalar_tensor_tensor(neg_p[:], neg_a[:], th_sb[:], log_rest[:], ALU.add, ALU.min, accum_out=neg_sum[:])
        weighted = sb.tile([P, SLOTS], F32, name="weighted")
        nc.vector.tensor_tensor(weighted[:, :HALF], c0[:, :HALF], size_rows[:, :HALF], ALU.mult)
        z = sb.tile([P, 1], F32, name="z")
        nc.vector.tensor_tensor(z[:], reserve_sb[:], neg_sum[:], ALU.subtract)
        nc.vector.tensor_tensor(weighted[:, HALF:], c0[:, HALF:], size_rows[:, HALF:], ALU.mult)
        inv_z = sb.tile([P, 1], F32, name="inv_z")
        nc.vector.reciprocal(inv_z[:], z[:])
        terms = sb.tile([P, SLOTS], F32, name="terms")
        shift = sb.tile([P, 1], F32, name="shift")
        nc.vector.scalar_tensor_tensor(terms[:], weighted[:], inv_z[:], neg_p[:], ALU.mult, ALU.mult, accum_out=shift[:])
        dp = sb.tile([P, SLOTS], F32, name="dp")
        nc.vector.tensor_scalar(dp[:], weighted[:], shift[:], inv_z[:], ALU.add, ALU.mult)
        nc.vector.tensor_tensor(placed[:].indirect(offsets[:]), dp[:], slope[:], ALU.mult)

        result = sb.tile([P, T], F32, name="result")
        start = 0
        for n, width in enumerate(CHUNKS):
            cols = slice(start, start + width)
            nc.vector.tensor_tensor(result[:, cols], old_sb[:, cols], placed[:, cols], ALU.add)
            queue = nc.sync if n % 2 == 0 else nc.scalar
            queue.dma_start(out[:, cols], result[:, cols])
            start += width
